import numpy as np
import ml_dtypes


def mxq(x, axis, fmt="e4m3"):
    dtype, down = {"e4m3": (ml_dtypes.float8_e4m3fn, 7), "e5m2": (ml_dtypes.float8_e5m2, 14)}[fmt]
    v = np.moveaxis(np.asarray(x, np.float32).astype(ml_dtypes.bfloat16).astype(np.float64), axis, -1)
    blocks = v.reshape(v.shape[:-1] + (-1, 32))
    amax = np.abs(blocks).max(-1, keepdims=True)
    byte = np.maximum(np.where(amax > 0, np.frexp(amax)[1] - 1 + 127, 0) - down, 1)
    scale = np.exp2(byte - 127.0)
    codes = (blocks / scale).astype(np.float32).astype(dtype).astype(np.float64)
    return np.moveaxis((codes * scale).reshape(v.shape), -1, axis)


WIDE = False


def mx_kscale(k):
    if not WIDE:
        return np.ones(k)
    levels = np.array([30, -30])
    if k % 512:
        return np.exp2(np.random.permutation(np.resize(levels, k // 32))).repeat(32)
    a = np.empty((k // 512, 16))
    for p in range(k // 512):
        a[p, :8] = np.random.permutation(np.resize(levels, 8))
        for g in range(8):
            far = levels[np.abs(levels - a[p, g]) >= 10]
            a[p, g + 8] = far[np.random.randint(len(far))]
    return np.exp2(a.ravel()).repeat(32)


def f64(x):
    return np.asarray(x).astype(np.float64)


def striped(idx):
    return np.tile(np.asarray(idx).reshape(-1, 16).T, (8, 1)).astype(np.uint16)


def unstriped(offs):
    return offs[:16].T.reshape(-1).astype(np.int64)


E2M1 = np.array([0.0, 0.5, 1.0, 1.5, 2.0, 3.0, 4.0, 6.0, -0.0, -0.5, -1.0, -1.5, -2.0, -3.0, -4.0, -6.0])


def pack_weight(w, fmt):
    k, n = w.shape
    w = f64(np.asarray(w, np.float32).astype(ml_dtypes.bfloat16)).reshape(k // 32, 32, n)
    amax = np.abs(w).max(1)
    if fmt in ("e4m3", "e5m2"):
        byte = np.frexp(amax)[1] - 1 + 127 - (7 if fmt == "e4m3" else 14)
    else:
        mant, ex = np.frexp(amax / 6.0)
        byte = np.where(mant > 0.5, ex, ex - 1) + 127
    byte = np.clip(np.where(amax > 0, byte, 1), 1, 254)
    scaled = (w * np.exp2(127.0 - byte)[:, None, :]).reshape(k, n).astype(np.float32)
    by_word = np.ascontiguousarray(scaled.reshape(k // 512, 128, 4, n).transpose(0, 1, 3, 2))
    if fmt in ("e4m3", "e5m2"):
        words = by_word.astype(ml_dtypes.float8_e4m3fn if fmt == "e4m3" else ml_dtypes.float8_e5m2).view(np.uint8)
    else:
        c = by_word.astype(ml_dtypes.float4_e2m1fn).view(np.uint8) & 0xF
        words = (c[..., 0::2] | (c[..., 1::2] << 4)).reshape(k // 512, 128, 2 * n)
    return np.ascontiguousarray(words), np.ascontiguousarray(byte.astype(np.uint8).reshape(k // 512, 16, n))


def unpack_weight(words, scales, fmt):
    g, _, n = scales.shape
    words = np.ascontiguousarray(words).reshape(g, 128, n, -1)
    if fmt in ("e4m3", "e5m2"):
        vals = words.view(ml_dtypes.float8_e4m3fn if fmt == "e4m3" else ml_dtypes.float8_e5m2).astype(np.float64)
    else:
        nib = np.empty((g, 128, n, 4), np.uint8)
        nib[..., 0::2] = words & 0xF
        nib[..., 1::2] = words >> 4
        vals = E2M1[nib]
    vals = vals * np.repeat(np.exp2(scales.astype(np.float64) - 127.0), 8, axis=1)[..., None]
    return vals.transpose(0, 1, 3, 2).reshape(g * 512, n)


K, T, J, R, V, N = 1024, 1024, 256, 512, 512, 256


def setup_inputs():
    n = np.random.standard_normal
    idx = np.random.permutation(T)[:J]
    idx2 = np.random.permutation(V)[:J]
    fk = mx_kscale(K)
    fr = mx_kscale(R)
    xtp = pack_weight(n((K, T)) / fk[:, None], "e5m2")
    wp = pack_weight(n((K, R)) * 1 / np.sqrt(K) * fk[:, None] * fr, "e4m3")
    wbp = pack_weight(n((R, N)) * 1 / np.sqrt(R) / fr[:, None], "e2m1")
    return {
        "xt_words": xtp[0],
        "xt_scales": xtp[1],
        "w_words": wp[0],
        "w_scales": wp[1],
        "tb": (n((R, V)) * 0.7 * fr[:, None]).astype(np.float32),
        "wb_words": wbp[0],
        "wb_scales": wbp[1],
        "bi": (np.random.uniform(-0.5, 0.5, (1, N))).astype(np.float32),
        "offs": striped(idx),
        "offs2": striped(idx2),
    }


def reference(xt_words, xt_scales, w_words, w_scales, tb, wb_words, wb_scales, bi, offs, offs2):
    idx = unstriped(offs)
    idx2 = unstriped(offs2)
    xtu = unpack_weight(xt_words, xt_scales, "e5m2")
    wu = unpack_weight(w_words, w_scales, "e4m3")
    wbu = unpack_weight(wb_words, wb_scales, "e2m1")
    xtidxg = xtu[:, idx]
    a = wu.T @ xtidxg
    hid = np.maximum(a - f64(tb)[:, idx2], 0.0)
    hidq = mxq(hid, 0, "e5m2")
    p = hidq.T @ wbu
    ea = np.exp(0.7 * p + f64(bi))
    y = 256.0 * ea / np.sum(ea, axis=1, keepdims=True)
    return y

@@ -1,0 +1,163 @@
+from contextlib import ExitStack
+
+import concourse.mybir as mybir
+from concourse.masks import make_identity
+
+K, T, J, R, V, N = 1024, 1024, 256, 512, 512, 256
+FLOPS = 2 * K * R * J + 2 * R * J * N
+
+F32 = mybir.dt.float32
+BF16 = mybir.dt.bfloat16
+I32 = mybir.dt.int32
+U32 = mybir.dt.uint32
+U16 = mybir.dt.uint16
+U8 = mybir.dt.uint8
+E4M3 = mybir.dt.float8_e4m3fn_x4
+E5M2 = mybir.dt.float8_e5m2_x4
+E2M1 = mybir.dt.float4_e2m1fn_x4
+ALU = mybir.AluOpType
+ACT = mybir.ActivationFunctionType
+
+P = 128
+PACK = 4
+PASSES = K // (P * PACK)
+HALVES = J // P
+
+
+def load_scale_rows(queue, plane, scales):
+    for r in range(4):
+        queue.dma_start(
+            out=plane[r:P:32, :, :].bitcast(I32),
+            in_=scales[:, r:16:4, :].rearrange("z q c -> q z c").bitcast(I32),
+        )
+
+
+def tile_list_picked_overtable_rowshares_kernel(
+    tc, xt_words, xt_scales, w_words, w_scales, tb, wb_words, wb_scales, bi, offs, offs2, out
+):
+    nc = tc.nc
+    with ExitStack() as ctx:
+        sb = ctx.enter_context(tc.tile_pool(name="sb", bufs=1))
+        ps = ctx.enter_context(tc.psum_pool(name="ps", bufs=1))
+
+        tokens = sb.tile([P, J // 16], U16, name="tokens")
+        entries = sb.tile([P, J // 16], U16, name="entries")
+        xs = sb.tile([P, PASSES, T], U8, name="xs", align_bytes=64)
+        ws = sb.tile([P, PASSES, R], U8, name="ws", align_bytes=64)
+        wbs = sb.tile([P, 1, N], U8, name="wbs", align_bytes=64)
+        xw = [sb.tile([P, T], U32, name=f"xw{z}", align_bytes=64) for z in range(PASSES)]
+        ww = [sb.tile([P, R], U32, name=f"ww{z}", align_bytes=64) for z in range(PASSES)]
+        tbl = [sb.tile([P, V], F32, name=f"tbl{t}", align_bytes=64) for t in range(PACK)]
+        wbw = sb.tile([P, 2 * N], U8, name="wbw", align_bytes=64)
+        bcol = sb.tile([P, 2], F32, name="bcol")
+        ident = sb.tile([P, P], F32, name="ident")
+
+        nc.gpsimd.memset(xs[:, 0, :].bitcast(I32), 0)
+        nc.vector.memset(xs[:, 1, :].bitcast(I32), 0)
+        nc.vector.memset(ws[:].rearrange("p z c -> p (z c)").bitcast(I32), 0)
+        nc.vector.memset(wbs[:].rearrange("p z c -> p (z c)").bitcast(I32), 0)
+
+        w_rows = [w_words[z].rearrange("p c t -> p (c t)").bitcast(I32) for z in range(PASSES)]
+        xt_rows = [xt_words[z].rearrange("p c t -> p (c t)").bitcast(I32) for z in range(PASSES)]
+        nc.sync.dma_start(tokens[:], offs)
+        nc.sync.dma_start(out=ww[0][:].bitcast(I32), in_=w_rows[0])
+        load_scale_rows(nc.sync, xs, xt_scales)
+        nc.sync.dma_start(out=xw[0][:].bitcast(I32), in_=xt_rows[0])
+        nc.sync.dma_start(out=ww[1][:].bitcast(I32), in_=w_rows[1])
+        load_scale_rows(nc.sync, ws, w_scales)
+        nc.sync.dma_start(out=xw[1][:].bitcast(I32), in_=xt_rows[1])
+        nc.sync.dma_start(entries[:], offs2)
+        tb_rows = tb.rearrange("(p t) v -> p t v", t=PACK)
+        for t in range(PACK):
+            nc.sync.dma_start(out=tbl[t][:], in_=tb_rows[:, t, :])
+        nc.sync.dma_start(out=wbw[:].bitcast(I32), in_=wb_words[0].bitcast(I32))
+        load_scale_rows(nc.sync, wbs, wb_scales)
+        make_identity(nc, ident[:])
+        nc.gpsimd.dma_start(out=bcol[:], in_=bi[0].rearrange("(p c) -> p c", c=2))
+        bias_ps = ps.tile([P, 2, P], F32, name="bias_ps")
+        for c in range(2):
+            nc.tensor.transpose(bias_ps[:, c, :], bcol[:, c : c + 1].to_broadcast([P, P]), ident[:])
+        bias = sb.tile([P, P, 2], F32, name="bias")
+        nc.scalar.copy(out=bias[:], in_=bias_ps[:].rearrange("m c p -> m p c"))
+
+        wp = [sb.tile([P, PACK, P], U32, name=f"wp{z}", align_bytes=64) for z in range(PASSES)]
+        wsp = [sb.tile([P, PACK, P], U8, name=f"wsp{z}", align_bytes=64) for z in range(PASSES)]
+        xg = [sb.tile([P, J], U32, name=f"xg{z}", align_bytes=64) for z in range(PASSES)]
+        xsg = [sb.tile([P, J], U8, name=f"xsg{z}", align_bytes=64) for z in range(PASSES)]
+        a_ps = [ps.tile([P, J], F32, name=f"a_ps{t}") for t in range(PACK)]
+        for z in range(PASSES):
+            nc.vector.tensor_copy(
+                out=wsp[z][:].rearrange("p t (c i) -> p c t i", i=16),
+                in_=ws[:, z, :].rearrange("p (c i t) -> p c t i", i=16, t=PACK),
+            )
+            nc.vector.tensor_copy(xg[z][:], xw[z][:].indirect(tokens[:]))
+            nc.vector.tensor_copy(xsg[z][:], xs[:, z, :].indirect(tokens[:]))
+            nc.vector.tensor_copy(
+                out=wp[z][:].rearrange("p t (c i) -> p c t i", i=4),
+                in_=ww[z][:].rearrange("p (c i t) -> p c t i", i=4, t=PACK),
+            )
+            for t in range(PACK):
+                nc.tensor.matmul_mx(
+                    out=a_ps[t][:],
+                    lhsT=wp[z][:, t, :].bitcast(E4M3),
+                    lhsT_scale=wsp[z][:, t, :],
+                    rhs=xg[z][:].bitcast(E5M2),
+                    rhs_scale=xsg[z][:],
+                    start=(z == 0),
+                    stop=(z == PASSES - 1),
+                )
+
+        diff = sb.tile([P, PACK, J], F32, name="diff")
+        last = [sb.tile([P, P], F32, name=f"last{h}") for h in range(HALVES)]
+        cols = P // 16
+        nc.vector.tensor_copy(last[0][:], tbl[PACK - 1][:].indirect(entries[:, 0:cols]))
+        for t in range(PACK - 1):
+            picked = sb.tile([P, J], F32, name=f"picked{t}")
+            nc.scalar.activation(picked[:], tbl[t][:].indirect(entries[:]), ACT.Copy)
+            nc.vector.tensor_tensor(diff[:, t, :], a_ps[t][:], picked[:], ALU.subtract)
+        t = PACK - 1
+        nc.scalar.activation(last[1][:], tbl[t][:].indirect(entries[:, cols : 2 * cols]), ACT.Copy)
+        for h in range(HALVES):
+            js = slice(h * P, (h + 1) * P)
+            nc.vector.tensor_tensor(diff[:, t, js], a_ps[t][:, js], last[h][:], ALU.subtract)
+
+        hid = [sb.tile([P, P, PACK], BF16, name=f"hid{h}", align_bytes=64) for h in range(HALVES)]
+        src = [diff[:, :, h * P : (h + 1) * P].rearrange("p t j -> p j t") for h in range(HALVES)]
+        nc.vector.tensor_scalar_max(hid[0][:], src[0], 0.0)
+        nc.scalar.activation(hid[1][:], src[1], ACT.Relu)
+
+        p_ps = []
+        for h in range(HALVES):
+            codes = sb.tile([P, P], U32, name=f"codes{h}", align_bytes=64)
+            scales = sb.tile([P, P], U8, name=f"scales{h}", align_bytes=64)
+            nc.vector.quantize_mx(
+                out=codes[:].bitcast(E5M2), scales=scales[:], in_=hid[h][:].rearrange("p j t -> p (j t)")
+            )
+            p_ps.append(ps.tile([P, N], F32, name=f"p_ps{h}"))
+            nc.tensor.matmul_mx(
+                out=p_ps[h][:],
+                lhsT=codes[:].bitcast(E5M2),
+                lhsT_scale=scales[:],
+                rhs=wbw[:].bitcast(E2M1),
+                rhs_scale=wbs[:, 0, :],
+                start=True,
+                stop=True,
+            )
+
+        logits = [sb.tile([P, N], F32, name=f"logits{h}") for h in range(HALVES)]
+        neg_max = [sb.tile([P, 1], F32, name=f"neg_max{h}") for h in range(HALVES)]
+        expd = [sb.tile([P, N], F32, name=f"expd{h}") for h in range(HALVES)]
+        total = [sb.tile([P, 1], F32, name=f"total{h}") for h in range(HALVES)]
+        inv = [sb.tile([P, 1], F32, name=f"inv{h}") for h in range(HALVES)]
+        res = [sb.tile([P, N], F32, name=f"res{h}") for h in range(HALVES)]
+        for h in range(HALVES):
+            nc.vector.scalar_tensor_tensor(
+                logits[h][:], p_ps[h][:], 0.7, bias[:].rearrange("m p c -> m (p c)"), ALU.mult, ALU.add
+            )
+        for h in range(HALVES):
+            nc.vector.tensor_reduce(neg_max[h][:], logits[h][:], mybir.AxisListType.X, ALU.max, negate=True)
+            nc.scalar.activation(expd[h][:], logits[h][:], ACT.Exp, bias=neg_max[h][:], accum_out=total[h][:])
+        for h in range(HALVES):
+            nc.vector.reciprocal(inv[h][:], total[h][:])
+            nc.vector.tensor_scalar(res[h][:], expd[h][:], inv[h][:], 256.0, ALU.mult, ALU.mult)
+            nc.sync.dma_start(out=out[h * P : (h + 1) * P, :], in_=res[h][:])

@@ -52,21 +52,20 @@ def tile_list_picked_overtable_rowshares_kernel(
         bcol = sb.tile([P, 2], F32, name="bcol")
         ident = sb.tile([P, P], F32, name="ident")
 
-        nc.gpsimd.memset(xs[:, 0, :].bitcast(I32), 0)
-        nc.vector.memset(xs[:, 1, :].bitcast(I32), 0)
         nc.vector.memset(ws[:].rearrange("p z c -> p (z c)").bitcast(I32), 0)
+        nc.vector.memset(xs[:].rearrange("p z c -> p (z c)").bitcast(I32), 0)
         nc.vector.memset(wbs[:].rearrange("p z c -> p (z c)").bitcast(I32), 0)
 
         w_rows = [w_words[z].rearrange("p c t -> p (c t)").bitcast(I32) for z in range(PASSES)]
         xt_rows = [xt_words[z].rearrange("p c t -> p (c t)").bitcast(I32) for z in range(PASSES)]
         nc.sync.dma_start(tokens[:], offs)
+        nc.sync.dma_start(entries[:], offs2)
         nc.sync.dma_start(out=ww[0][:].bitcast(I32), in_=w_rows[0])
-        load_scale_rows(nc.sync, xs, xt_scales)
+        load_scale_rows(nc.sync, ws, w_scales)
         nc.sync.dma_start(out=xw[0][:].bitcast(I32), in_=xt_rows[0])
         nc.sync.dma_start(out=ww[1][:].bitcast(I32), in_=w_rows[1])
-        load_scale_rows(nc.sync, ws, w_scales)
+        load_scale_rows(nc.sync, xs, xt_scales)
         nc.sync.dma_start(out=xw[1][:].bitcast(I32), in_=xt_rows[1])
-        nc.sync.dma_start(entries[:], offs2)
         tb_rows = tb.rearrange("(p t) v -> p t v", t=PACK)
         for t in range(PACK):
             nc.sync.dma_start(out=tbl[t][:], in_=tb_rows[:, t, :])
@@ -110,15 +109,14 @@ def tile_list_picked_overtable_rowshares_kernel(
         diff = sb.tile([P, PACK, J], F32, name="diff")
         last = [sb.tile([P, P], F32, name=f"last{h}") for h in range(HALVES)]
         cols = P // 16
-        nc.vector.tensor_copy(last[0][:], tbl[PACK - 1][:].indirect(entries[:, 0:cols]))
         for t in range(PACK - 1):
             picked = sb.tile([P, J], F32, name=f"picked{t}")
             nc.scalar.activation(picked[:], tbl[t][:].indirect(entries[:]), ACT.Copy)
             nc.vector.tensor_tensor(diff[:, t, :], a_ps[t][:], picked[:], ALU.subtract)
         t = PACK - 1
-        nc.scalar.activation(last[1][:], tbl[t][:].indirect(entries[:, cols : 2 * cols]), ACT.Copy)
         for h in range(HALVES):
             js = slice(h * P, (h + 1) * P)
+            nc.scalar.activation(last[h][:], tbl[t][:].indirect(entries[:, h * cols : (h + 1) * cols]), ACT.Copy)
             nc.vector.tensor_tensor(diff[:, t, js], a_ps[t][:, js], last[h][:], ALU.subtract)
 
         hid = [sb.tile([P, P, PACK], BF16, name=f"hid{h}", align_bytes=64) for h in range(HALVES)]

@@ -22,6 +22,7 @@ P = 128
 PACK = 4
 PASSES = K // (P * PACK)
 HALVES = J // P
+SPLIT = 64
 
 
 def load_scale_rows(queue, plane, scales):
@@ -58,15 +59,15 @@ def tile_list_picked_overtable_rowshares_kernel(
 
         w_rows = [w_words[z].rearrange("p c t -> p (c t)").bitcast(I32) for z in range(PASSES)]
         xt_rows = [xt_words[z].rearrange("p c t -> p (c t)").bitcast(I32) for z in range(PASSES)]
-        nc.sync.dma_start(tokens[:], offs)
-        nc.sync.dma_start(entries[:], offs2)
+        tb_rows = tb.rearrange("(p t) v -> p t v", t=PACK)
         nc.sync.dma_start(out=ww[0][:].bitcast(I32), in_=w_rows[0])
+        nc.sync.dma_start(tokens[:], offs)
         load_scale_rows(nc.sync, ws, w_scales)
         nc.sync.dma_start(out=xw[0][:].bitcast(I32), in_=xt_rows[0])
         nc.sync.dma_start(out=ww[1][:].bitcast(I32), in_=w_rows[1])
         load_scale_rows(nc.sync, xs, xt_scales)
         nc.sync.dma_start(out=xw[1][:].bitcast(I32), in_=xt_rows[1])
-        tb_rows = tb.rearrange("(p t) v -> p t v", t=PACK)
+        nc.sync.dma_start(entries[:], offs2)
         for t in range(PACK):
             nc.sync.dma_start(out=tbl[t][:], in_=tb_rows[:, t, :])
         nc.sync.dma_start(out=wbw[:].bitcast(I32), in_=wb_words[0].bitcast(I32))
@@ -122,7 +123,8 @@ def tile_list_picked_overtable_rowshares_kernel(
         hid = [sb.tile([P, P, PACK], BF16, name=f"hid{h}", align_bytes=64) for h in range(HALVES)]
         src = [diff[:, :, h * P : (h + 1) * P].rearrange("p t j -> p j t") for h in range(HALVES)]
         nc.vector.tensor_scalar_max(hid[0][:], src[0], 0.0)
-        nc.scalar.activation(hid[1][:], src[1], ACT.Relu)
+        nc.scalar.activation(hid[1][:, 0:SPLIT, :], src[1][:, 0:SPLIT, :], ACT.Relu)
+        nc.vector.tensor_scalar_max(hid[1][:, SPLIT:P, :], src[1][:, SPLIT:P, :], 0.0)
 
         p_ps = []
         for h in range(HALVES):

from contextlib import ExitStack

import concourse.mybir as mybir
from concourse.masks import make_identity

K, T, J, R, V, N = 1024, 1024, 256, 512, 512, 256
FLOPS = 2 * K * R * J + 2 * R * J * N

F32 = mybir.dt.float32
BF16 = mybir.dt.bfloat16
I32 = mybir.dt.int32
U32 = mybir.dt.uint32
U16 = mybir.dt.uint16
U8 = mybir.dt.uint8
E4M3 = mybir.dt.float8_e4m3fn_x4
E5M2 = mybir.dt.float8_e5m2_x4
E2M1 = mybir.dt.float4_e2m1fn_x4
ALU = mybir.AluOpType
ACT = mybir.ActivationFunctionType

P = 128
PACK = 4
PASSES = K // (P * PACK)
HALVES = J // P
SPLIT = 64


def load_scale_rows(queue, plane, scales):
    for r in range(4):
        queue.dma_start(
            out=plane[r:P:32, :, :].bitcast(I32),
            in_=scales[:, r:16:4, :].rearrange("z q c -> q z c").bitcast(I32),
        )


def tile_list_picked_overtable_rowshares_kernel(
    tc, xt_words, xt_scales, w_words, w_scales, tb, wb_words, wb_scales, bi, offs, offs2, out
):
    nc = tc.nc
    with ExitStack() as ctx:
        sb = ctx.enter_context(tc.tile_pool(name="sb", bufs=1))
        ps = ctx.enter_context(tc.psum_pool(name="ps", bufs=1))

        tokens = sb.tile([P, J // 16], U16, name="tokens")
        entries = sb.tile([P, J // 16], U16, name="entries")
        xs = sb.tile([P, PASSES, T], U8, name="xs", align_bytes=64)
        ws = sb.tile([P, PASSES, R], U8, name="ws", align_bytes=64)
        wbs = sb.tile([P, 1, N], U8, name="wbs", align_bytes=64)
        xw = [sb.tile([P, T], U32, name=f"xw{z}", align_bytes=64) for z in range(PASSES)]
        ww = [sb.tile([P, R], U32, name=f"ww{z}", align_bytes=64) for z in range(PASSES)]
        tbl = [sb.tile([P, V], F32, name=f"tbl{t}", align_bytes=64) for t in range(PACK)]
        wbw = sb.tile([P, 2 * N], U8, name="wbw", align_bytes=64)
        bcol = sb.tile([P, 2], F32, name="bcol")
        ident = sb.tile([P, P], F32, name="ident")

        nc.vector.memset(ws[:].rearrange("p z c -> p (z c)").bitcast(I32), 0)
        nc.vector.memset(xs[:].rearrange("p z c -> p (z c)").bitcast(I32), 0)
        nc.vector.memset(wbs[:].rearrange("p z c -> p (z c)").bitcast(I32), 0)

        w_rows = [w_words[z].rearrange("p c t -> p (c t)").bitcast(I32) for z in range(PASSES)]
        xt_rows = [xt_words[z].rearrange("p c t -> p (c t)").bitcast(I32) for z in range(PASSES)]
        tb_rows = tb.rearrange("(p t) v -> p t v", t=PACK)
        nc.sync.dma_start(out=ww[0][:].bitcast(I32), in_=w_rows[0])
        nc.sync.dma_start(tokens[:], offs)
        load_scale_rows(nc.sync, ws, w_scales)
        nc.sync.dma_start(out=xw[0][:].bitcast(I32), in_=xt_rows[0])
        nc.sync.dma_start(out=ww[1][:].bitcast(I32), in_=w_rows[1])
        load_scale_rows(nc.sync, xs, xt_scales)
        nc.sync.dma_start(out=xw[1][:].bitcast(I32), in_=xt_rows[1])
        nc.sync.dma_start(entries[:], offs2)
        for t in range(PACK):
            nc.sync.dma_start(out=tbl[t][:], in_=tb_rows[:, t, :])
        nc.sync.dma_start(out=wbw[:].bitcast(I32), in_=wb_words[0].bitcast(I32))
        load_scale_rows(nc.sync, wbs, wb_scales)
        make_identity(nc, ident[:])
        nc.gpsimd.dma_start(out=bcol[:], in_=bi[0].rearrange("(p c) -> p c", c=2))
        bias_ps = ps.tile([P, 2, P], F32, name="bias_ps")
        for c in range(2):
            nc.tensor.transpose(bias_ps[:, c, :], bcol[:, c : c + 1].to_broadcast([P, P]), ident[:])
        bias = sb.tile([P, P, 2], F32, name="bias")
        nc.scalar.copy(out=bias[:], in_=bias_ps[:].rearrange("m c p -> m p c"))

        wp = [sb.tile([P, PACK, P], U32, name=f"wp{z}", align_bytes=64) for z in range(PASSES)]
        wsp = [sb.tile([P, PACK, P], U8, name=f"wsp{z}", align_bytes=64) for z in range(PASSES)]
        xg = [sb.tile([P, J], U32, name=f"xg{z}", align_bytes=64) for z in range(PASSES)]
        xsg = [sb.tile([P, J], U8, name=f"xsg{z}", align_bytes=64) for z in range(PASSES)]
        a_ps = [ps.tile([P, J], F32, name=f"a_ps{t}") for t in range(PACK)]
        for z in range(PASSES):
            nc.vector.tensor_copy(
                out=wsp[z][:].rearrange("p t (c i) -> p c t i", i=16),
                in_=ws[:, z, :].rearrange("p (c i t) -> p c t i", i=16, t=PACK),
            )
            nc.vector.tensor_copy(xg[z][:], xw[z][:].indirect(tokens[:]))
            nc.vector.tensor_copy(xsg[z][:], xs[:, z, :].indirect(tokens[:]))
            nc.vector.tensor_copy(
                out=wp[z][:].rearrange("p t (c i) -> p c t i", i=4),
                in_=ww[z][:].rearrange("p (c i t) -> p c t i", i=4, t=PACK),
            )
            for t in range(PACK):
                nc.tensor.matmul_mx(
                    out=a_ps[t][:],
                    lhsT=wp[z][:, t, :].bitcast(E4M3),
                    lhsT_scale=wsp[z][:, t, :],
                    rhs=xg[z][:].bitcast(E5M2),
                    rhs_scale=xsg[z][:],
                    start=(z == 0),
                    stop=(z == PASSES - 1),
                )

        diff = sb.tile([P, PACK, J], F32, name="diff")
        last = [sb.tile([P, P], F32, name=f"last{h}") for h in range(HALVES)]
        cols = P // 16
        for t in range(PACK - 1):
            picked = sb.tile([P, J], F32, name=f"picked{t}")
            nc.scalar.activation(picked[:], tbl[t][:].indirect(entries[:]), ACT.Copy)
            nc.vector.tensor_tensor(diff[:, t, :], a_ps[t][:], picked[:], ALU.subtract)
        t = PACK - 1
        for h in range(HALVES):
            js = slice(h * P, (h + 1) * P)
            nc.scalar.activation(last[h][:], tbl[t][:].indirect(entries[:, h * cols : (h + 1) * cols]), ACT.Copy)
            nc.vector.tensor_tensor(diff[:, t, js], a_ps[t][:, js], last[h][:], ALU.subtract)

        hid = [sb.tile([P, P, PACK], BF16, name=f"hid{h}", align_bytes=64) for h in range(HALVES)]
        src = [diff[:, :, h * P : (h + 1) * P].rearrange("p t j -> p j t") for h in range(HALVES)]
        nc.vector.tensor_scalar_max(hid[0][:], src[0], 0.0)
        nc.scalar.activation(hid[1][:, 0:SPLIT, :], src[1][:, 0:SPLIT, :], ACT.Relu)
        nc.vector.tensor_scalar_max(hid[1][:, SPLIT:P, :], src[1][:, SPLIT:P, :], 0.0)

        p_ps = []
        for h in range(HALVES):
            codes = sb.tile([P, P], U32, name=f"codes{h}", align_bytes=64)
            scales = sb.tile([P, P], U8, name=f"scales{h}", align_bytes=64)
            nc.vector.quantize_mx(
                out=codes[:].bitcast(E5M2), scales=scales[:], in_=hid[h][:].rearrange("p j t -> p (j t)")
            )
            p_ps.append(ps.tile([P, N], F32, name=f"p_ps{h}"))
            nc.tensor.matmul_mx(
                out=p_ps[h][:],
                lhsT=codes[:].bitcast(E5M2),
                lhsT_scale=scales[:],
                rhs=wbw[:].bitcast(E2M1),
                rhs_scale=wbs[:, 0, :],
                start=True,
                stop=True,
            )

        logits = [sb.tile([P, N], F32, name=f"logits{h}") for h in range(HALVES)]
        neg_max = [sb.tile([P, 1], F32, name=f"neg_max{h}") for h in range(HALVES)]
        expd = [sb.tile([P, N], F32, name=f"expd{h}") for h in range(HALVES)]
        total = [sb.tile([P, 1], F32, name=f"total{h}") for h in range(HALVES)]
        inv = [sb.tile([P, 1], F32, name=f"inv{h}") for h in range(HALVES)]
        res = [sb.tile([P, N], F32, name=f"res{h}") for h in range(HALVES)]
        for h in range(HALVES):
            nc.vector.scalar_tensor_tensor(
                logits[h][:], p_ps[h][:], 0.7, bias[:].rearrange("m p c -> m (p c)"), ALU.mult, ALU.add
            )
        for h in range(HALVES):
            nc.vector.tensor_reduce(neg_max[h][:], logits[h][:], mybir.AxisListType.X, ALU.max, negate=True)
            nc.scalar.activation(expd[h][:], logits[h][:], ACT.Exp, bias=neg_max[h][:], accum_out=total[h][:])
        for h in range(HALVES):
            nc.vector.reciprocal(inv[h][:], total[h][:])
            nc.vector.tensor_scalar(res[h][:], expd[h][:], inv[h][:], 256.0, ALU.mult, ALU.mult)
            nc.sync.dma_start(out=out[h * P : (h + 1) * P, :], in_=res[h][:])
